import numpy as np
import ml_dtypes


def mxq(x, axis, fmt="e4m3"):
    dtype, down = {"e4m3": (ml_dtypes.float8_e4m3fn, 7), "e5m2": (ml_dtypes.float8_e5m2, 14)}[fmt]
    v = np.moveaxis(np.asarray(x, np.float32).astype(ml_dtypes.bfloat16).astype(np.float64), axis, -1)
    blocks = v.reshape(v.shape[:-1] + (-1, 32))
    amax = np.abs(blocks).max(-1, keepdims=True)
    byte = np.maximum(np.where(amax > 0, np.frexp(amax)[1] - 1 + 127, 0) - down, 1)
    scale = np.exp2(byte - 127.0)
    codes = (blocks / scale).astype(np.float32).astype(dtype).astype(np.float64)
    return np.moveaxis((codes * scale).reshape(v.shape), -1, axis)


WIDE = False


def mx_kscale(k):
    if not WIDE:
        return np.ones(k)
    levels = np.array([18, -18])
    if k % 512:
        return np.exp2(np.random.permutation(np.resize(levels, k // 32))).repeat(32)
    a = np.empty((k // 512, 16))
    for p in range(k // 512):
        a[p, :8] = np.random.permutation(np.resize(levels, 8))
        for g in range(8):
            far = levels[np.abs(levels - a[p, g]) >= 10]
            a[p, g + 8] = far[np.random.randint(len(far))]
    return np.exp2(a.ravel()).repeat(32)


def f64(x):
    return np.asarray(x).astype(np.float64)


def striped(idx):
    return np.tile(np.asarray(idx).reshape(-1, 16).T, (8, 1)).astype(np.uint16)


def unstriped(offs):
    return offs[:16].T.reshape(-1).astype(np.int64)


E2M1 = np.array([0.0, 0.5, 1.0, 1.5, 2.0, 3.0, 4.0, 6.0, -0.0, -0.5, -1.0, -1.5, -2.0, -3.0, -4.0, -6.0])


def pack_weight(w, fmt):
    k, n = w.shape
    w = f64(np.asarray(w, np.float32).astype(ml_dtypes.bfloat16)).reshape(k // 32, 32, n)
    amax = np.abs(w).max(1)
    if fmt == "e4m3":
        byte = np.frexp(amax)[1] - 1 + 127 - 7
    else:
        mant, ex = np.frexp(amax / 6.0)
        byte = np.where(mant > 0.5, ex, ex - 1) + 127
    byte = np.clip(np.where(amax > 0, byte, 1), 1, 254)
    scaled = (w * np.exp2(127.0 - byte)[:, None, :]).reshape(k, n).astype(np.float32)
    by_word = np.ascontiguousarray(scaled.reshape(k // 512, 128, 4, n).transpose(0, 1, 3, 2))
    if fmt == "e4m3":
        words = by_word.astype(ml_dtypes.float8_e4m3fn).view(np.uint8)
    else:
        c = by_word.astype(ml_dtypes.float4_e2m1fn).view(np.uint8) & 0xF
        words = (c[..., 0::2] | (c[..., 1::2] << 4)).reshape(k // 512, 128, 2 * n)
    return np.ascontiguousarray(words), np.ascontiguousarray(byte.astype(np.uint8).reshape(k // 512, 16, n))


def unpack_weight(words, scales, fmt):
    g, _, n = scales.shape
    words = np.ascontiguousarray(words).reshape(g, 128, n, -1)
    if fmt == "e4m3":
        vals = words.view(ml_dtypes.float8_e4m3fn).astype(np.float64)
    else:
        nib = np.empty((g, 128, n, 4), np.uint8)
        nib[..., 0::2] = words & 0xF
        nib[..., 1::2] = words >> 4
        vals = E2M1[nib]
    vals = vals * np.repeat(np.exp2(scales.astype(np.float64) - 127.0), 8, axis=1)[..., None]
    return vals.transpose(0, 1, 3, 2).reshape(g * 512, n)


def planes(y):
    n, m = y.shape
    v = y.astype(np.float32).astype(ml_dtypes.bfloat16).astype(np.float64).reshape(n // 32, 32, m)
    top = np.abs(v).max(1)
    byte = np.clip(np.where(top > 0, np.frexp(top)[1] - 1 + 127 - 7, 1), 1, 254)
    codes = (v * np.exp2(127.0 - byte)[:, None, :]).reshape(n, m).astype(np.float32).astype(ml_dtypes.float8_e4m3fn).view(np.uint8)
    words = codes.reshape(n // 512, 128, 4, m).transpose(0, 1, 3, 2)
    return np.ascontiguousarray(words), np.ascontiguousarray(byte.astype(np.uint8).reshape(n // 512, 16, m))


T, C, D, DV = 1024, 1024, 512, 1024
BETA = 0.25


def setup_inputs():
    n = np.random.standard_normal
    grid = lambda v: np.clip(np.round(v * 16) / 16, -4, 4)
    v = mx_kscale(DV)[:, None]
    wp = pack_weight(n((DV, D)) / np.sqrt(DV) / v, "e2m1")
    return {
        "zT": (grid(n((DV, T))) * v).astype(np.float32),
        "cb": (grid(n((DV, C))) * v).astype(np.float32),
        "w_words": wp[0],
        "w_scales": wp[1],
        "offs": striped(np.random.randint(0, C, T)),
    }


def reference(zT, cb, w_words, w_scales, offs):
    e = f64(zT) - f64(cb)[:, unstriped(offs)]
    g = BETA * e
    out_0 = unpack_weight(w_words, w_scales, "e2m1").T @ mxq(g, 0, "e5m2")
    return (out_0,) + planes(out_0)

@@ -1,0 +1,190 @@
+from contextlib import ExitStack
+
+import concourse.mybir as mybir
+
+T, C, D, DV = 1024, 1024, 512, 1024
+BETA = 0.25
+FLOPS = 2 * DV * D * T
+
+F32 = mybir.dt.float32
+BF16 = mybir.dt.bfloat16
+I32 = mybir.dt.int32
+U32 = mybir.dt.uint32
+U16 = mybir.dt.uint16
+U8 = mybir.dt.uint8
+E4M3X4 = mybir.dt.float8_e4m3fn_x4
+E5M2X4 = mybir.dt.float8_e5m2_x4
+E2M1X4 = mybir.dt.float4_e2m1fn_x4
+COPY = mybir.ActivationFunctionType.Copy
+SUB = mybir.AluOpType.subtract
+MULT = mybir.AluOpType.mult
+
+P = 128
+L = 4
+H = 512
+
+
+def weave_views(dst, src):
+    return (
+        dst.rearrange("p (c i) j -> p c j i", i=4),
+        src.rearrange("p j (c i) -> p c j i", i=4),
+    )
+
+
+def tile_attend_gvq_pl_c_x_kernel(tc, zT, cb, w_words, w_scales, offs, out_0, out_1, out_2):
+    nc = tc.nc
+    with ExitStack() as ctx:
+        keep = ctx.enter_context(tc.tile_pool(name="keep", bufs=1))
+        psum = ctx.enter_context(tc.psum_pool(name="psum", bufs=1))
+
+        cb_rows = cb.rearrange("(o p j) c -> o j p c", o=2, j=L)
+        z_rows = zT.rearrange("(o p j) t -> o p j t", o=2, j=L)
+        out_rows = out_0.rearrange("(p j) t -> p j t", j=L)
+
+        offsets = keep.tile([P, T // 16], U16, name="offsets")
+        nc.sync.dma_start(offsets[:], offs)
+
+        book = {}
+        zt = {}
+
+        def load_book(o, j):
+            book[o, j] = keep.tile([P, C], F32, name=f"book{o}{j}")
+            nc.sync.dma_start(book[o, j][:], cb_rows[o, j])
+
+        def load_z(o, j):
+            tile = keep.tile([P, T], F32, name=f"z{o}{j}")
+            nc.sync.dma_start(tile[:], z_rows[o, :, j, :])
+            zt[o, j, 0] = tile[:, 0:H]
+            zt[o, j, 1] = tile[:, H:T]
+
+        def load_z_half(o, j, h):
+            tile = keep.tile([P, H], F32, name=f"z{o}{j}{h}")
+            nc.sync.dma_start(tile[:], z_rows[o, :, j, h * H:(h + 1) * H])
+            zt[o, j, h] = tile[:]
+
+        load_book(0, 0)
+        w_raw = keep.tile([P, 2, 2 * D], U8, name="w_raw")
+        nc.scalar.dma_start(w_raw[:].bitcast(I32), w_words.rearrange("o p b -> p o b").bitcast(I32))
+        ws_raw = keep.tile([P, 2, D], U8, name="ws_raw")
+        nc.vector.memset(ws_raw[:].bitcast(I32), 0)
+        for q in range(4):
+            nc.scalar.dma_start(
+                ws_raw[32 * q:32 * q + 4, :, :].bitcast(I32),
+                w_scales[:, 4 * q:4 * q + 4, :].rearrange("o f d -> f o d").bitcast(I32),
+            )
+        load_z(0, 0)
+        for o, j in [(0, 1), (0, 2), (0, 3), (1, 0), (1, 1)]:
+            load_book(o, j)
+            load_z(o, j)
+        load_book(1, 2)
+        load_book(1, 3)
+        for h in range(2):
+            load_z_half(1, 2, h)
+            load_z_half(1, 3, h)
+
+        w_dealt = keep.tile([P, 2, 2 * D], U8, name="w_dealt", align_bytes=64)
+        nc.vector.tensor_copy(
+            w_dealt[:].bitcast(U16).rearrange("p o (j c i) -> p o c j i", j=L, i=8),
+            w_raw[:].bitcast(U16).rearrange("p o (c i j) -> p o c j i", j=L, i=8),
+        )
+        ws_dealt = keep.tile([P, 2, D], U8, name="ws_dealt", align_bytes=64)
+        nc.vector.tensor_copy(
+            ws_dealt[:].rearrange("p o (j c i) -> p o c j i", j=L, i=16),
+            ws_raw[:].rearrange("p o (c i j) -> p o c j i", j=L, i=16),
+        )
+
+        banks = [[psum.tile([P, H], F32, name=f"bank{h}{j}") for j in range(L)] for h in range(2)]
+        err = {(o, h): keep.tile([P, L, H], F32, name=f"err{o}{h}") for o in range(2) for h in range(2)}
+        gw = {(o, h): keep.tile([P, H, L], BF16, name=f"gw{o}{h}", align_bytes=64) for o in range(2) for h in range(2)}
+        gc = {(o, h): keep.tile([P, H], U32, name=f"gc{o}{h}", align_bytes=64) for o in range(2) for h in range(2)}
+        gs = {(o, h): keep.tile([P, H], U8, name=f"gs{o}{h}", align_bytes=64) for o in range(2) for h in range(2)}
+        picked = {}
+
+        def look_up(o, j, h, reuse=None):
+            picked[o, j, h] = picked[reuse] if reuse else keep.tile([P, H], F32, name=f"picked{o}{j}{h}")
+            nc.vector.tensor_copy(picked[o, j, h][:], book[o, j][:].indirect(offsets[:, h * 32:(h + 1) * 32]))
+
+        def subtract(o, j, h, eng):
+            eng.tensor_tensor(err[o, h][:, j, :], zt[o, j, h], picked[o, j, h][:], SUB)
+
+        def weave_g(o, h, a, b, on_vector):
+            dst, src = weave_views(gw[o, h][:, a:b, :], err[o, h][:, :, a:b])
+            if on_vector:
+                nc.vector.tensor_scalar(dst, src, BETA, None, MULT)
+            else:
+                nc.scalar.activation(dst, src, COPY, scale=BETA)
+
+        def quantise_g(o, h):
+            nc.vector.quantize_mx(gc[o, h][:].bitcast(E5M2X4), gs[o, h][:], gw[o, h][:].rearrange("p t j -> p (t j)"))
+
+        def multiply(o, h):
+            for j in range(L):
+                nc.tensor.matmul_mx(
+                    banks[h][j][:],
+                    lhsT=w_dealt[:, o, 2 * P * j:2 * P * (j + 1)].bitcast(E2M1X4),
+                    lhsT_scale=ws_dealt[:, o, P * j:P * (j + 1)],
+                    rhs=gc[o, h][:].bitcast(E5M2X4),
+                    rhs_scale=gs[o, h][:],
+                    start=(o == 0),
+                    stop=(o == 1),
+                )
+
+        y_codes = keep.tile([P, T], U32, name="y_codes", align_bytes=64)
+        y_scales = keep.tile([P, T], U8, name="y_scales", align_bytes=64)
+        codes_out = out_1[0].rearrange("p t b -> p (t b)").bitcast(I32)
+
+        def finish(h, evac, weave):
+            y = keep.tile([P, L, H], F32, name=f"y{h}")
+            yw = keep.tile([P, H, L], BF16, name=f"yw{h}", align_bytes=64)
+            for j in range(L):
+                if evac[j] == "v":
+                    nc.vector.tensor_copy(y[:, j, :], banks[h][j][:])
+                else:
+                    nc.scalar.copy(y[:, j, :], banks[h][j][:])
+                if j % 2 == 1:
+                    nc.sync.dma_start(out_rows[:, j - 1:j + 1, h * H:(h + 1) * H], y[:, j - 1:j + 1, :])
+            for k in range(2):
+                a, b = k * 256, (k + 1) * 256
+                dst, src = weave_views(yw[:, a:b, :], y[:, :, a:b])
+                if weave[k] == "v":
+                    nc.vector.tensor_copy(dst, src)
+                else:
+                    nc.scalar.copy(dst, src)
+                nc.vector.quantize_mx(
+                    y_codes[:, h * H + a:h * H + b].bitcast(E4M3X4),
+                    y_scales[:, h * H + a:h * H + b],
+                    yw[:, a:b, :].rearrange("p t j -> p (t j)"),
+                )
+            nc.sync.dma_start(codes_out[:, h * H:(h + 1) * H], y_codes[:, h * H:(h + 1) * H].bitcast(I32))
+
+        for j in range(L):
+            for h in range(2):
+                look_up(0, j, h)
+                subtract(0, j, h, nc.gpsimd)
+        for h in range(2):
+            weave_g(0, h, 0, H, False)
+        for j in range(2):
+            for h in range(2):
+                look_up(1, j, h)
+                subtract(1, j, h, nc.gpsimd)
+        for h in range(2):
+            quantise_g(0, h)
+            multiply(0, h)
+        for j in (2, 3):
+            look_up(1, j, 0)
+            subtract(1, j, 0, nc.gpsimd)
+        weave_g(1, 0, 0, H, False)
+        look_up(1, 2, 1, reuse=(1, 1, 0))
+        subtract(1, 2, 1, nc.vector)
+        look_up(1, 3, 1, reuse=(1, 1, 1))
+        subtract(1, 3, 1, nc.vector)
+        quantise_g(1, 0)
+        multiply(1, 0)
+        weave_g(1, 1, 0, H, True)
+        quantise_g(1, 1)
+        multiply(1, 1)
+        finish(0, "ssss", "ss")
+        finish(1, "vsvs", "vs")
+        for q in range(4):
+            eng = nc.sync if q % 2 == 0 else nc.scalar
+            eng.dma_start(out_2[0, 4 * q:4 * q + 4, :].bitcast(I32), y_scales[32 * q:32 * q + 4, :].bitcast(I32))

@@ -1,6 +1,7 @@
 from contextlib import ExitStack
 
 import concourse.mybir as mybir
+from concourse.masks import make_identity
 
 T, C, D, DV = 1024, 1024, 512, 1024
 BETA = 0.25
@@ -46,6 +47,9 @@ def tile_attend_gvq_pl_c_x_kernel(tc, zT, cb, w_words, w_scales, offs, out_0, ou
 
         book = {}
         zt = {}
+        zwhole = {}
+        zpair = {}
+        zneg = {}
 
         def load_book(o, j):
             book[o, j] = keep.tile([P, C], F32, name=f"book{o}{j}")
@@ -54,6 +58,7 @@ def tile_attend_gvq_pl_c_x_kernel(tc, zT, cb, w_words, w_scales, offs, out_0, ou
         def load_z(o, j):
             tile = keep.tile([P, T], F32, name=f"z{o}{j}")
             nc.sync.dma_start(tile[:], z_rows[o, :, j, :])
+            zwhole[o, j] = tile
             zt[o, j, 0] = tile[:, 0:H]
             zt[o, j, 1] = tile[:, H:T]
 
@@ -72,15 +77,26 @@ def tile_attend_gvq_pl_c_x_kernel(tc, zT, cb, w_words, w_scales, offs, out_0, ou
                 ws_raw[32 * q:32 * q + 4, :, :].bitcast(I32),
                 w_scales[:, 4 * q:4 * q + 4, :].rearrange("o f d -> f o d").bitcast(I32),
             )
+        ident = keep.tile([P, P], F32, name="ident")
+        make_identity(nc, ident[:])
         load_z(0, 0)
-        for o, j in [(0, 1), (0, 2), (0, 3), (1, 0), (1, 1)]:
-            load_book(o, j)
-            load_z(o, j)
-        load_book(1, 2)
-        load_book(1, 3)
-        for h in range(2):
-            load_z_half(1, 2, h)
-            load_z_half(1, 3, h)
+        for j in (1, 2, 3):
+            load_book(0, j)
+            load_z(0, j)
+
+        def load_z_pair(u, h):
+            tile = keep.tile([P, 2, H], F32, name=f"z1{u}{h}")
+            nc.sync.dma_start(tile[:], z_rows[1, :, 2 * u:2 * u + 2, h * H:(h + 1) * H])
+            zpair[u, h] = tile
+            for e in range(2):
+                zt[1, 2 * u + e, h] = tile[:, e, :]
+
+        for u in range(2):
+            load_book(1, 2 * u)
+            load_book(1, 2 * u + 1)
+            load_z_pair(u, 0)
+        for u in range(2):
+            load_z_pair(u, 1)
 
         w_dealt = keep.tile([P, 2, 2 * D], U8, name="w_dealt", align_bytes=64)
         nc.vector.tensor_copy(
@@ -94,14 +110,63 @@ def tile_attend_gvq_pl_c_x_kernel(tc, zT, cb, w_words, w_scales, offs, out_0, ou
         )
 
         banks = [[psum.tile([P, H], F32, name=f"bank{h}{j}") for j in range(L)] for h in range(2)]
-        err = {(o, h): keep.tile([P, L, H], F32, name=f"err{o}{h}") for o in range(2) for h in range(2)}
-        gw = {(o, h): keep.tile([P, H, L], BF16, name=f"gw{o}{h}", align_bytes=64) for o in range(2) for h in range(2)}
-        gc = {(o, h): keep.tile([P, H], U32, name=f"gc{o}{h}", align_bytes=64) for o in range(2) for h in range(2)}
+        err = {(1, h): keep.tile([P, L, H], F32, name=f"err1{h}") for h in range(2)}
+        gw = {(o, h): keep.tile([P, H, L], BF16, name=f"gw{o}{h}", tag=f"gw{o}{h}", align_bytes=64) for o in range(2) for h in range(2)}
+        turned = {}
+        count = [0, 0]
+
+        def negate_whole(o, j):
+            tile = keep.tile([P, T], F32, name=f"zneg{o}{j}")
+            nc.scalar.activation(tile[:], zwhole[o, j][:], COPY, scale=-1.0)
+            zneg[o, j, 0] = tile[:, 0:H]
+            zneg[o, j, 1] = tile[:, H:T]
+
+        def negate_pair(u, h):
+            tile = keep.tile([P, 2, H], F32, name=f"zneg1{u}{h}")
+            nc.scalar.activation(tile[:], zpair[u, h][:], COPY, scale=-1.0)
+            for e in range(2):
+                zneg[1, 2 * u + e, h] = tile[:, e, :]
+
+        def turn_and_add(o, u, h):
+            for b in range(2):
+                if u == 0:
+                    turned[o, h, b] = keep.tile([P, 2, 2, P, 2], BF16, name=f"turned{o}{h}{b}", tag=f"turned{o}{h}{b}", align_bytes=64)
+                bank = banks[1][count[0] % 2]
+                count[0] = count[0] + 1
+                for s in range(2):
+                    cols = slice(256 * b + P * s, 256 * b + P * (s + 1))
+                    for e in range(2):
+                        dst = bank[:, P * (2 * s + e):P * (2 * s + e + 1)]
+                        nc.tensor.matmul(dst, zneg[o, 2 * u + e, h][:, cols], ident[:], start=True, stop=False, is_transpose=True)
+                        nc.tensor.matmul(dst, picked[o, 2 * u + e, h][:, cols], ident[:], start=False, stop=True, is_transpose=True)
+                nc.scalar.activation(
+                    turned[o, h, b][:, :, u, :, :], bank[:].rearrange("t (s e p) -> t s p e", s=2, e=2), COPY, scale=-BETA
+                )
+
+        def turn_back(o, h):
+            words = gw[o, h][:].rearrange("p t j -> p (t j)").bitcast(F32)
+            for b in range(2):
+                bank = banks[1][2 + count[1] % 2]
+                count[1] = count[1] + 1
+                src = turned[o, h, b][:].rearrange("t s u p e -> t (s u p e)").bitcast(F32)
+                for s in range(2):
+                    for u in range(2):
+                        nc.tensor.transpose(
+                            bank[:, 256 * u + P * s:256 * u + P * (s + 1)],
+                            src[:, P * (2 * s + u):P * (2 * s + u + 1)],
+                            ident[:],
+                        )
+                nc.scalar.copy(
+                    words[:, H * b:H * (b + 1)].rearrange("p (t u) -> p t u", u=2),
+                    bank[:].rearrange("p (u t) -> p t u", u=2),
+                )
+
+        gc = {}
         gs = {(o, h): keep.tile([P, H], U8, name=f"gs{o}{h}", align_bytes=64) for o in range(2) for h in range(2)}
         picked = {}
 
-        def look_up(o, j, h, reuse=None):
-            picked[o, j, h] = picked[reuse] if reuse else keep.tile([P, H], F32, name=f"picked{o}{j}{h}")
+        def look_up(o, j, h, tag=None):
+            picked[o, j, h] = keep.tile([P, H], F32, name=f"picked{o}{j}{h}", tag=tag or f"picked{o}{j}{h}", align_bytes=64)
             nc.vector.tensor_copy(picked[o, j, h][:], book[o, j][:].indirect(offsets[:, h * 32:(h + 1) * 32]))
 
         def subtract(o, j, h, eng):
@@ -114,7 +179,8 @@ def tile_attend_gvq_pl_c_x_kernel(tc, zT, cb, w_words, w_scales, offs, out_0, ou
             else:
                 nc.scalar.activation(dst, src, COPY, scale=BETA)
 
-        def quantise_g(o, h):
+        def quantise_g(o, h, tag=None):
+            gc[o, h] = keep.tile([P, H], U32, name=f"gc{o}{h}", tag=tag or f"gc{o}{h}", align_bytes=64)
             nc.vector.quantize_mx(gc[o, h][:].bitcast(E5M2X4), gs[o, h][:], gw[o, h][:].rearrange("p t j -> p (t j)"))
 
         def multiply(o, h):
@@ -141,8 +207,7 @@ def tile_attend_gvq_pl_c_x_kernel(tc, zT, cb, w_words, w_scales, offs, out_0, ou
                     nc.vector.tensor_copy(y[:, j, :], banks[h][j][:])
                 else:
                     nc.scalar.copy(y[:, j, :], banks[h][j][:])
-                if j % 2 == 1:
-                    nc.sync.dma_start(out_rows[:, j - 1:j + 1, h * H:(h + 1) * H], y[:, j - 1:j + 1, :])
+                nc.sync.dma_start(out_rows[:, j, h * H:(h + 1) * H], y[:, j, :])
             for k in range(2):
                 a, b = k * 256, (k + 1) * 256
                 dst, src = weave_views(yw[:, a:b, :], y[:, :, a:b])
@@ -157,33 +222,43 @@ def tile_attend_gvq_pl_c_x_kernel(tc, zT, cb, w_words, w_scales, offs, out_0, ou
                 )
             nc.sync.dma_start(codes_out[:, h * H:(h + 1) * H], y_codes[:, h * H:(h + 1) * H].bitcast(I32))
 
-        for j in range(L):
+        for u in range(2):
+            for j in (2 * u, 2 * u + 1):
+                negate_whole(0, j)
+                for h in range(2):
+                    look_up(0, j, h)
             for h in range(2):
-                look_up(0, j, h)
-                subtract(0, j, h, nc.gpsimd)
+                turn_and_add(0, u, h)
         for h in range(2):
-            weave_g(0, h, 0, H, False)
-        for j in range(2):
-            for h in range(2):
-                look_up(1, j, h)
-                subtract(1, j, h, nc.gpsimd)
-        for h in range(2):
-            quantise_g(0, h)
-            multiply(0, h)
-        for j in (2, 3):
-            look_up(1, j, 0)
-            subtract(1, j, 0, nc.gpsimd)
+            turn_back(0, h)
+        look_up(1, 0, 0)
+        look_up(1, 1, 0)
+        subtract(1, 0, 0, nc.vector)
+        look_up(1, 2, 0)
+        subtract(1, 1, 0, nc.vector)
+        look_up(1, 3, 0)
+        quantise_g(0, 0)
+        multiply(0, 0)
+        subtract(1, 2, 0, nc.vector)
+        subtract(1, 3, 0, nc.vector)
         weave_g(1, 0, 0, H, False)
-        look_up(1, 2, 1, reuse=(1, 1, 0))
-        subtract(1, 2, 1, nc.vector)
-        look_up(1, 3, 1, reuse=(1, 1, 1))
-        subtract(1, 3, 1, nc.vector)
+        look_up(1, 0, 1, tag="picked120")
+        look_up(1, 1, 1, tag="picked130")
+        subtract(1, 0, 1, nc.vector)
         quantise_g(1, 0)
         multiply(1, 0)
-        weave_g(1, 1, 0, H, True)
+        finish(0, "ssss", "ss")
+        look_up(1, 2, 1, tag="gw10")
+        subtract(1, 1, 1, nc.vector)
+        look_up(1, 3, 1, tag="picked120")
+        quantise_g(0, 1, tag="picked130")
+        multiply(0, 1)
+        subtract(1, 2, 1, nc.vector)
+        subtract(1, 3, 1, nc.vector)
+        weave_g(1, 1, 0, 192, False)
+        weave_g(1, 1, 192, H, True)
         quantise_g(1, 1)
         multiply(1, 1)
-        finish(0, "ssss", "ss")
         finish(1, "vsvs", "vs")
         for q in range(4):
             eng = nc.sync if q % 2 == 0 else nc.scalar

@@ -71,9 +71,9 @@ def tile_attend_gvq_pl_c_x_kernel(tc, zT, cb, w_words, w_scales, offs, out_0, ou
         w_raw = keep.tile([P, 2, 2 * D], U8, name="w_raw")
         nc.scalar.dma_start(w_raw[:].bitcast(I32), w_words.rearrange("o p b -> p o b").bitcast(I32))
         ws_raw = keep.tile([P, 2, D], U8, name="ws_raw")
-        nc.vector.memset(ws_raw[:].bitcast(I32), 0)
+        nc.gpsimd.memset(ws_raw[:].bitcast(I32), 0)
         for q in range(4):
-            nc.scalar.dma_start(
+            nc.sync.dma_start(
                 ws_raw[32 * q:32 * q + 4, :, :].bitcast(I32),
                 w_scales[:, 4 * q:4 * q + 4, :].rearrange("o f d -> f o d").bitcast(I32),
             )
@@ -110,7 +110,7 @@ def tile_attend_gvq_pl_c_x_kernel(tc, zT, cb, w_words, w_scales, offs, out_0, ou
         )
 
         banks = [[psum.tile([P, H], F32, name=f"bank{h}{j}") for j in range(L)] for h in range(2)]
-        err = {(1, h): keep.tile([P, L, H], F32, name=f"err1{h}") for h in range(2)}
+        err = {}
         gw = {(o, h): keep.tile([P, H, L], BF16, name=f"gw{o}{h}", tag=f"gw{o}{h}", align_bytes=64) for o in range(2) for h in range(2)}
         turned = {}
         count = [0, 0]
@@ -131,7 +131,7 @@ def tile_attend_gvq_pl_c_x_kernel(tc, zT, cb, w_words, w_scales, offs, out_0, ou
             for b in range(2):
                 if u == 0:
                     turned[o, h, b] = keep.tile([P, 2, 2, P, 2], BF16, name=f"turned{o}{h}{b}", tag=f"turned{o}{h}{b}", align_bytes=64)
-                bank = banks[1][count[0] % 2]
+                bank = banks[1][count[0] % 4]
                 count[0] = count[0] + 1
                 for s in range(2):
                     cols = slice(256 * b + P * s, 256 * b + P * (s + 1))
@@ -146,7 +146,7 @@ def tile_attend_gvq_pl_c_x_kernel(tc, zT, cb, w_words, w_scales, offs, out_0, ou
         def turn_back(o, h):
             words = gw[o, h][:].rearrange("p t j -> p (t j)").bitcast(F32)
             for b in range(2):
-                bank = banks[1][2 + count[1] % 2]
+                bank = banks[0][count[1] % 4]
                 count[1] = count[1] + 1
                 src = turned[o, h, b][:].rearrange("t s u p e -> t (s u p e)").bitcast(F32)
                 for s in range(2):
@@ -199,15 +199,29 @@ def tile_attend_gvq_pl_c_x_kernel(tc, zT, cb, w_words, w_scales, offs, out_0, ou
         y_scales = keep.tile([P, T], U8, name="y_scales", align_bytes=64)
         codes_out = out_1[0].rearrange("p t b -> p (t b)").bitcast(I32)
 
+        woven = {}
+
+        def quantise_y(h, k):
+            a, b = k * 256, (k + 1) * 256
+            nc.vector.quantize_mx(
+                y_codes[:, h * H + a:h * H + b].bitcast(E4M3X4),
+                y_scales[:, h * H + a:h * H + b],
+                woven[h][:, a:b, :].rearrange("p t j -> p (t j)"),
+            )
+            if k == 1:
+                nc.sync.dma_start(codes_out[:, h * H:(h + 1) * H], y_codes[:, h * H:(h + 1) * H].bitcast(I32))
+
         def finish(h, evac, weave):
             y = keep.tile([P, L, H], F32, name=f"y{h}")
             yw = keep.tile([P, H, L], BF16, name=f"yw{h}", align_bytes=64)
+            woven[h] = yw
             for j in range(L):
                 if evac[j] == "v":
                     nc.vector.tensor_copy(y[:, j, :], banks[h][j][:])
                 else:
                     nc.scalar.copy(y[:, j, :], banks[h][j][:])
-                nc.sync.dma_start(out_rows[:, j, h * H:(h + 1) * H], y[:, j, :])
+                if j % 2 == 1:
+                    nc.sync.dma_start(out_rows[:, j - 1:j + 1, h * H:(h + 1) * H], y[:, j - 1:j + 1, :])
             for k in range(2):
                 a, b = k * 256, (k + 1) * 256
                 dst, src = weave_views(yw[:, a:b, :], y[:, :, a:b])
@@ -215,12 +229,6 @@ def tile_attend_gvq_pl_c_x_kernel(tc, zT, cb, w_words, w_scales, offs, out_0, ou
                     nc.vector.tensor_copy(dst, src)
                 else:
                     nc.scalar.copy(dst, src)
-                nc.vector.quantize_mx(
-                    y_codes[:, h * H + a:h * H + b].bitcast(E4M3X4),
-                    y_scales[:, h * H + a:h * H + b],
-                    yw[:, a:b, :].rearrange("p t j -> p (t j)"),
-                )
-            nc.sync.dma_start(codes_out[:, h * H:(h + 1) * H], y_codes[:, h * H:(h + 1) * H].bitcast(I32))
 
         for u in range(2):
             for j in (2 * u, 2 * u + 1):
@@ -229,37 +237,41 @@ def tile_attend_gvq_pl_c_x_kernel(tc, zT, cb, w_words, w_scales, offs, out_0, ou
                     look_up(0, j, h)
             for h in range(2):
                 turn_and_add(0, u, h)
-        for h in range(2):
-            turn_back(0, h)
         look_up(1, 0, 0)
         look_up(1, 1, 0)
-        subtract(1, 0, 0, nc.vector)
+        negate_pair(0, 0)
+        turn_and_add(1, 0, 0)
+        turn_back(0, 0)
         look_up(1, 2, 0)
-        subtract(1, 1, 0, nc.vector)
         look_up(1, 3, 0)
+        negate_pair(1, 0)
+        turn_and_add(1, 1, 0)
+        turn_back(1, 0)
+        turn_back(0, 1)
+        err[1, 1] = keep.tile([P, L, H], F32, name="err11")
+        look_up(1, 0, 1, tag="picked031")
+        look_up(1, 1, 1, tag="picked100")
+        subtract(1, 0, 1, nc.vector)
+        subtract(1, 1, 1, nc.vector)
         quantise_g(0, 0)
         multiply(0, 0)
-        subtract(1, 2, 0, nc.vector)
-        subtract(1, 3, 0, nc.vector)
-        weave_g(1, 0, 0, H, False)
-        look_up(1, 0, 1, tag="picked120")
-        look_up(1, 1, 1, tag="picked130")
-        subtract(1, 0, 1, nc.vector)
+        look_up(1, 2, 1, tag="gw00")
         quantise_g(1, 0)
         multiply(1, 0)
         finish(0, "ssss", "ss")
-        look_up(1, 2, 1, tag="gw10")
-        subtract(1, 1, 1, nc.vector)
-        look_up(1, 3, 1, tag="picked120")
-        quantise_g(0, 1, tag="picked130")
-        multiply(0, 1)
+        look_up(1, 3, 1, tag="gw10")
         subtract(1, 2, 1, nc.vector)
         subtract(1, 3, 1, nc.vector)
-        weave_g(1, 1, 0, 192, False)
-        weave_g(1, 1, 192, H, True)
+        quantise_g(0, 1, tag="gw00")
+        multiply(0, 1)
+        weave_g(1, 1, 0, H, True)
         quantise_g(1, 1)
         multiply(1, 1)
+        quantise_y(0, 0)
+        quantise_y(0, 1)
         finish(1, "vsvs", "vs")
+        quantise_y(1, 0)
+        quantise_y(1, 1)
         for q in range(4):
             eng = nc.sync if q % 2 == 0 else nc.scalar
             eng.dma_start(out_2[0, 4 * q:4 * q + 4, :].bitcast(I32), y_scales[32 * q:32 * q + 4, :].bitcast(I32))

@@ -52,7 +52,7 @@ def tile_attend_gvq_pl_c_x_kernel(tc, zT, cb, w_words, w_scales, offs, out_0, ou
         zneg = {}
 
         def load_book(o, j):
-            book[o, j] = keep.tile([P, C], F32, name=f"book{o}{j}")
+            book[o, j] = keep.tile([P, C], F32, name=f"book{o}{j}", tag=f"book{o}{j}", align_bytes=64)
             nc.sync.dma_start(book[o, j][:], cb_rows[o, j])
 
         def load_z(o, j):
@@ -85,16 +85,17 @@ def tile_attend_gvq_pl_c_x_kernel(tc, zT, cb, w_words, w_scales, offs, out_0, ou
             load_z(0, j)
 
         def load_z_pair(u, h):
-            tile = keep.tile([P, 2, H], F32, name=f"z1{u}{h}")
+            tile = keep.tile([P, 2, H], F32, name=f"z1{u}{h}", tag=f"z1{u}{h}", align_bytes=64)
             nc.sync.dma_start(tile[:], z_rows[1, :, 2 * u:2 * u + 2, h * H:(h + 1) * H])
             zpair[u, h] = tile
             for e in range(2):
                 zt[1, 2 * u + e, h] = tile[:, e, :]
 
-        for u in range(2):
-            load_book(1, 2 * u)
-            load_book(1, 2 * u + 1)
-            load_z_pair(u, 0)
+        for j in range(3):
+            load_book(1, j)
+        load_z_pair(0, 0)
+        load_book(1, 3)
+        load_z_pair(1, 0)
         for u in range(2):
             load_z_pair(u, 1)
 
@@ -122,13 +123,13 @@ def tile_attend_gvq_pl_c_x_kernel(tc, zT, cb, w_words, w_scales, offs, out_0, ou
             zneg[o, j, 1] = tile[:, H:T]
 
         def negate_pair(u, h):
-            tile = keep.tile([P, 2, H], F32, name=f"zneg1{u}{h}")
-            nc.scalar.activation(tile[:], zpair[u, h][:], COPY, scale=-1.0)
+            tile = keep.tile([P, 2, 256], F32, name=f"zneg1{u}{h}")
+            nc.scalar.activation(tile[:], zpair[u, h][:, :, 0:256], COPY, scale=-1.0)
             for e in range(2):
                 zneg[1, 2 * u + e, h] = tile[:, e, :]
 
-        def turn_and_add(o, u, h):
-            for b in range(2):
+        def turn_and_add(o, u, h, blocks=(0, 1)):
+            for b in blocks:
                 if u == 0:
                     turned[o, h, b] = keep.tile([P, 2, 2, P, 2], BF16, name=f"turned{o}{h}{b}", tag=f"turned{o}{h}{b}", align_bytes=64)
                 bank = banks[1][count[0] % 4]
@@ -143,10 +144,10 @@ def tile_attend_gvq_pl_c_x_kernel(tc, zT, cb, w_words, w_scales, offs, out_0, ou
                     turned[o, h, b][:, :, u, :, :], bank[:].rearrange("t (s e p) -> t s p e", s=2, e=2), COPY, scale=-BETA
                 )
 
-        def turn_back(o, h):
+        def turn_back(o, h, blocks=(0, 1), where=None):
             words = gw[o, h][:].rearrange("p t j -> p (t j)").bitcast(F32)
-            for b in range(2):
-                bank = banks[0][count[1] % 4]
+            for b in blocks:
+                bank = where[b]
                 count[1] = count[1] + 1
                 src = turned[o, h, b][:].rearrange("t s u p e -> t (s u p e)").bitcast(F32)
                 for s in range(2):
@@ -168,6 +169,13 @@ def tile_attend_gvq_pl_c_x_kernel(tc, zT, cb, w_words, w_scales, offs, out_0, ou
         def look_up(o, j, h, tag=None):
             picked[o, j, h] = keep.tile([P, H], F32, name=f"picked{o}{j}{h}", tag=tag or f"picked{o}{j}{h}", align_bytes=64)
             nc.vector.tensor_copy(picked[o, j, h][:], book[o, j][:].indirect(offsets[:, h * 32:(h + 1) * 32]))
+
+        def look_up_pair(u):
+            tile = keep.tile([P, 2, H], F32, name=f"pickedpair{u}", tag=f"pickedpair{u}", align_bytes=64)
+            for e in range(2):
+                picked[1, 2 * u + e, 0] = tile[:, e, :]
+                nc.vector.tensor_copy(tile[:, e, :], book[1, 2 * u + e][:].indirect(offsets[:, 0:32]))
+            nc.vector.tensor_tensor(err[1, 0][:, 2 * u:2 * u + 2, 256:H], zpair[u, 0][:, :, 256:H], tile[:, :, 256:H], SUB)
 
         def subtract(o, j, h, eng):
             eng.tensor_tensor(err[o, h][:, j, :], zt[o, j, h], picked[o, j, h][:], SUB)
@@ -195,21 +203,18 @@ def tile_attend_gvq_pl_c_x_kernel(tc, zT, cb, w_words, w_scales, offs, out_0, ou
                     stop=(o == 1),
                 )
 
-        y_codes = keep.tile([P, T], U32, name="y_codes", align_bytes=64)
         y_scales = keep.tile([P, T], U8, name="y_scales", align_bytes=64)
         codes_out = out_1[0].rearrange("p t b -> p (t b)").bitcast(I32)
 
         woven = {}
 
-        def quantise_y(h, k):
+        def quantise_y(h, k, codes):
             a, b = k * 256, (k + 1) * 256
             nc.vector.quantize_mx(
-                y_codes[:, h * H + a:h * H + b].bitcast(E4M3X4),
+                codes.bitcast(E4M3X4),
                 y_scales[:, h * H + a:h * H + b],
                 woven[h][:, a:b, :].rearrange("p t j -> p (t j)"),
             )
-            if k == 1:
-                nc.sync.dma_start(codes_out[:, h * H:(h + 1) * H], y_codes[:, h * H:(h + 1) * H].bitcast(I32))
 
         def finish(h, evac, weave):
             y = keep.tile([P, L, H], F32, name=f"y{h}")
@@ -237,41 +242,45 @@ def tile_attend_gvq_pl_c_x_kernel(tc, zT, cb, w_words, w_scales, offs, out_0, ou
                     look_up(0, j, h)
             for h in range(2):
                 turn_and_add(0, u, h)
-        look_up(1, 0, 0)
-        look_up(1, 1, 0)
+        err[1, 0] = keep.tile([P, L, H], F32, name="err10")
+        look_up_pair(0)
         negate_pair(0, 0)
-        turn_and_add(1, 0, 0)
-        turn_back(0, 0)
-        look_up(1, 2, 0)
-        look_up(1, 3, 0)
+        turn_and_add(1, 0, 0, (0,))
+        look_up_pair(1)
         negate_pair(1, 0)
-        turn_and_add(1, 1, 0)
-        turn_back(1, 0)
-        turn_back(0, 1)
-        err[1, 1] = keep.tile([P, L, H], F32, name="err11")
+        turn_and_add(1, 1, 0, (0,))
+        turn_back(0, 0, where=(banks[0][0], banks[0][1]))
+        weave_g(1, 0, 256, H, False)
+        turn_back(1, 0, (0,), where=(banks[0][2],))
+        turn_back(0, 1, where=(banks[0][3], banks[0][0]))
         look_up(1, 0, 1, tag="picked031")
-        look_up(1, 1, 1, tag="picked100")
-        subtract(1, 0, 1, nc.vector)
-        subtract(1, 1, 1, nc.vector)
+        look_up(1, 1, 1, tag="z110")
         quantise_g(0, 0)
         multiply(0, 0)
-        look_up(1, 2, 1, tag="gw00")
+        last = keep.tile([P, 2, H], F32, name="pickedlast", tag="gw00", align_bytes=64)
+        for e in range(2):
+            nc.vector.tensor_copy(last[:, e, :], book[1, 2 + e][:].indirect(offsets[:, 32:64]))
         quantise_g(1, 0)
         multiply(1, 0)
         finish(0, "ssss", "ss")
-        look_up(1, 3, 1, tag="gw10")
-        subtract(1, 2, 1, nc.vector)
-        subtract(1, 3, 1, nc.vector)
-        quantise_g(0, 1, tag="gw00")
+        err[1, 1] = keep.tile([P, L, H], F32, name="err11", tag="gw10", align_bytes=64)
+        subtract(1, 0, 1, nc.vector)
+        subtract(1, 1, 1, nc.vector)
+        nc.vector.tensor_tensor(err[1, 1][:, 2:4, :], zpair[1, 1][:], last[:], SUB)
+        quantise_g(0, 1, tag="z110")
         multiply(0, 1)
         weave_g(1, 1, 0, H, True)
         quantise_g(1, 1)
         multiply(1, 1)
-        quantise_y(0, 0)
-        quantise_y(0, 1)
         finish(1, "vsvs", "vs")
-        quantise_y(1, 0)
-        quantise_y(1, 1)
+        for k, tag in enumerate(("gw11", "gc11")):
+            codes = keep.tile([P, 256], U32, name=f"y_codes0{k}", tag=tag, align_bytes=64)
+            quantise_y(0, k, codes[:])
+            nc.sync.dma_start(codes_out[:, 256 * k:256 * (k + 1)], codes[:].bitcast(I32))
+        codes = keep.tile([P, H], U32, name="y_codes1", align_bytes=64)
+        for k in range(2):
+            quantise_y(1, k, codes[:, 256 * k:256 * (k + 1)])
+        nc.sync.dma_start(codes_out[:, H:T], codes[:].bitcast(I32))
         for q in range(4):
             eng = nc.sync if q % 2 == 0 else nc.scalar
             eng.dma_start(out_2[0, 4 * q:4 * q + 4, :].bitcast(I32), y_scales[32 * q:32 * q + 4, :].bitcast(I32))

from contextlib import ExitStack

import concourse.mybir as mybir
from concourse.masks import make_identity

T, C, D, DV = 1024, 1024, 512, 1024
BETA = 0.25
FLOPS = 2 * DV * D * T

F32 = mybir.dt.float32
BF16 = mybir.dt.bfloat16
I32 = mybir.dt.int32
U32 = mybir.dt.uint32
U16 = mybir.dt.uint16
U8 = mybir.dt.uint8
E4M3X4 = mybir.dt.float8_e4m3fn_x4
E5M2X4 = mybir.dt.float8_e5m2_x4
E2M1X4 = mybir.dt.float4_e2m1fn_x4
COPY = mybir.ActivationFunctionType.Copy
SUB = mybir.AluOpType.subtract
MULT = mybir.AluOpType.mult

P = 128
L = 4
H = 512


def weave_views(dst, src):
    return (
        dst.rearrange("p (c i) j -> p c j i", i=4),
        src.rearrange("p j (c i) -> p c j i", i=4),
    )


def tile_attend_gvq_pl_c_x_kernel(tc, zT, cb, w_words, w_scales, offs, out_0, out_1, out_2):
    nc = tc.nc
    with ExitStack() as ctx:
        keep = ctx.enter_context(tc.tile_pool(name="keep", bufs=1))
        psum = ctx.enter_context(tc.psum_pool(name="psum", bufs=1))

        cb_rows = cb.rearrange("(o p j) c -> o j p c", o=2, j=L)
        z_rows = zT.rearrange("(o p j) t -> o p j t", o=2, j=L)
        out_rows = out_0.rearrange("(p j) t -> p j t", j=L)

        offsets = keep.tile([P, T // 16], U16, name="offsets")
        nc.sync.dma_start(offsets[:], offs)

        book = {}
        zt = {}
        zwhole = {}
        zpair = {}
        zneg = {}

        def load_book(o, j):
            book[o, j] = keep.tile([P, C], F32, name=f"book{o}{j}", tag=f"book{o}{j}", align_bytes=64)
            nc.sync.dma_start(book[o, j][:], cb_rows[o, j])

        def load_z(o, j):
            tile = keep.tile([P, T], F32, name=f"z{o}{j}")
            nc.sync.dma_start(tile[:], z_rows[o, :, j, :])
            zwhole[o, j] = tile
            zt[o, j, 0] = tile[:, 0:H]
            zt[o, j, 1] = tile[:, H:T]

        def load_z_half(o, j, h):
            tile = keep.tile([P, H], F32, name=f"z{o}{j}{h}")
            nc.sync.dma_start(tile[:], z_rows[o, :, j, h * H:(h + 1) * H])
            zt[o, j, h] = tile[:]

        load_book(0, 0)
        w_raw = keep.tile([P, 2, 2 * D], U8, name="w_raw")
        nc.scalar.dma_start(w_raw[:].bitcast(I32), w_words.rearrange("o p b -> p o b").bitcast(I32))
        ws_raw = keep.tile([P, 2, D], U8, name="ws_raw")
        nc.gpsimd.memset(ws_raw[:].bitcast(I32), 0)
        for q in range(4):
            nc.sync.dma_start(
                ws_raw[32 * q:32 * q + 4, :, :].bitcast(I32),
                w_scales[:, 4 * q:4 * q + 4, :].rearrange("o f d -> f o d").bitcast(I32),
            )
        ident = keep.tile([P, P], F32, name="ident")
        make_identity(nc, ident[:])
        load_z(0, 0)
        for j in (1, 2, 3):
            load_book(0, j)
            load_z(0, j)

        def load_z_pair(u, h):
            tile = keep.tile([P, 2, H], F32, name=f"z1{u}{h}", tag=f"z1{u}{h}", align_bytes=64)
            nc.sync.dma_start(tile[:], z_rows[1, :, 2 * u:2 * u + 2, h * H:(h + 1) * H])
            zpair[u, h] = tile
            for e in range(2):
                zt[1, 2 * u + e, h] = tile[:, e, :]

        for j in range(3):
            load_book(1, j)
        load_z_pair(0, 0)
        load_book(1, 3)
        load_z_pair(1, 0)
        for u in range(2):
            load_z_pair(u, 1)

        w_dealt = keep.tile([P, 2, 2 * D], U8, name="w_dealt", align_bytes=64)
        nc.vector.tensor_copy(
            w_dealt[:].bitcast(U16).rearrange("p o (j c i) -> p o c j i", j=L, i=8),
            w_raw[:].bitcast(U16).rearrange("p o (c i j) -> p o c j i", j=L, i=8),
        )
        ws_dealt = keep.tile([P, 2, D], U8, name="ws_dealt", align_bytes=64)
        nc.vector.tensor_copy(
            ws_dealt[:].rearrange("p o (j c i) -> p o c j i", j=L, i=16),
            ws_raw[:].rearrange("p o (c i j) -> p o c j i", j=L, i=16),
        )

        banks = [[psum.tile([P, H], F32, name=f"bank{h}{j}") for j in range(L)] for h in range(2)]
        err = {}
        gw = {(o, h): keep.tile([P, H, L], BF16, name=f"gw{o}{h}", tag=f"gw{o}{h}", align_bytes=64) for o in range(2) for h in range(2)}
        turned = {}
        count = [0, 0]

        def negate_whole(o, j):
            tile = keep.tile([P, T], F32, name=f"zneg{o}{j}")
            nc.scalar.activation(tile[:], zwhole[o, j][:], COPY, scale=-1.0)
            zneg[o, j, 0] = tile[:, 0:H]
            zneg[o, j, 1] = tile[:, H:T]

        def negate_pair(u, h):
            tile = keep.tile([P, 2, 256], F32, name=f"zneg1{u}{h}")
            nc.scalar.activation(tile[:], zpair[u, h][:, :, 0:256], COPY, scale=-1.0)
            for e in range(2):
                zneg[1, 2 * u + e, h] = tile[:, e, :]

        def turn_and_add(o, u, h, blocks=(0, 1)):
            for b in blocks:
                if u == 0:
                    turned[o, h, b] = keep.tile([P, 2, 2, P, 2], BF16, name=f"turned{o}{h}{b}", tag=f"turned{o}{h}{b}", align_bytes=64)
                bank = banks[1][count[0] % 4]
                count[0] = count[0] + 1
                for s in range(2):
                    cols = slice(256 * b + P * s, 256 * b + P * (s + 1))
                    for e in range(2):
                        dst = bank[:, P * (2 * s + e):P * (2 * s + e + 1)]
                        nc.tensor.matmul(dst, zneg[o, 2 * u + e, h][:, cols], ident[:], start=True, stop=False, is_transpose=True)
                        nc.tensor.matmul(dst, picked[o, 2 * u + e, h][:, cols], ident[:], start=False, stop=True, is_transpose=True)
                nc.scalar.activation(
                    turned[o, h, b][:, :, u, :, :], bank[:].rearrange("t (s e p) -> t s p e", s=2, e=2), COPY, scale=-BETA
                )

        def turn_back(o, h, blocks=(0, 1), where=None):
            words = gw[o, h][:].rearrange("p t j -> p (t j)").bitcast(F32)
            for b in blocks:
                bank = where[b]
                count[1] = count[1] + 1
                src = turned[o, h, b][:].rearrange("t s u p e -> t (s u p e)").bitcast(F32)
                for s in range(2):
                    for u in range(2):
                        nc.tensor.transpose(
                            bank[:, 256 * u + P * s:256 * u + P * (s + 1)],
                            src[:, P * (2 * s + u):P * (2 * s + u + 1)],
                            ident[:],
                        )
                nc.scalar.copy(
                    words[:, H * b:H * (b + 1)].rearrange("p (t u) -> p t u", u=2),
                    bank[:].rearrange("p (u t) -> p t u", u=2),
                )

        gc = {}
        gs = {(o, h): keep.tile([P, H], U8, name=f"gs{o}{h}", align_bytes=64) for o in range(2) for h in range(2)}
        picked = {}

        def look_up(o, j, h, tag=None):
            picked[o, j, h] = keep.tile([P, H], F32, name=f"picked{o}{j}{h}", tag=tag or f"picked{o}{j}{h}", align_bytes=64)
            nc.vector.tensor_copy(picked[o, j, h][:], book[o, j][:].indirect(offsets[:, h * 32:(h + 1) * 32]))

        def look_up_pair(u):
            tile = keep.tile([P, 2, H], F32, name=f"pickedpair{u}", tag=f"pickedpair{u}", align_bytes=64)
            for e in range(2):
                picked[1, 2 * u + e, 0] = tile[:, e, :]
                nc.vector.tensor_copy(tile[:, e, :], book[1, 2 * u + e][:].indirect(offsets[:, 0:32]))
            nc.vector.tensor_tensor(err[1, 0][:, 2 * u:2 * u + 2, 256:H], zpair[u, 0][:, :, 256:H], tile[:, :, 256:H], SUB)

        def subtract(o, j, h, eng):
            eng.tensor_tensor(err[o, h][:, j, :], zt[o, j, h], picked[o, j, h][:], SUB)

        def weave_g(o, h, a, b, on_vector):
            dst, src = weave_views(gw[o, h][:, a:b, :], err[o, h][:, :, a:b])
            if on_vector:
                nc.vector.tensor_scalar(dst, src, BETA, None, MULT)
            else:
                nc.scalar.activation(dst, src, COPY, scale=BETA)

        def quantise_g(o, h, tag=None):
            gc[o, h] = keep.tile([P, H], U32, name=f"gc{o}{h}", tag=tag or f"gc{o}{h}", align_bytes=64)
            nc.vector.quantize_mx(gc[o, h][:].bitcast(E5M2X4), gs[o, h][:], gw[o, h][:].rearrange("p t j -> p (t j)"))

        def multiply(o, h):
            for j in range(L):
                nc.tensor.matmul_mx(
                    banks[h][j][:],
                    lhsT=w_dealt[:, o, 2 * P * j:2 * P * (j + 1)].bitcast(E2M1X4),
                    lhsT_scale=ws_dealt[:, o, P * j:P * (j + 1)],
                    rhs=gc[o, h][:].bitcast(E5M2X4),
                    rhs_scale=gs[o, h][:],
                    start=(o == 0),
                    stop=(o == 1),
                )

        y_scales = keep.tile([P, T], U8, name="y_scales", align_bytes=64)
        codes_out = out_1[0].rearrange("p t b -> p (t b)").bitcast(I32)

        woven = {}

        def quantise_y(h, k, codes):
            a, b = k * 256, (k + 1) * 256
            nc.vector.quantize_mx(
                codes.bitcast(E4M3X4),
                y_scales[:, h * H + a:h * H + b],
                woven[h][:, a:b, :].rearrange("p t j -> p (t j)"),
            )

        def finish(h, evac, weave):
            y = keep.tile([P, L, H], F32, name=f"y{h}")
            yw = keep.tile([P, H, L], BF16, name=f"yw{h}", align_bytes=64)
            woven[h] = yw
            for j in range(L):
                if evac[j] == "v":
                    nc.vector.tensor_copy(y[:, j, :], banks[h][j][:])
                else:
                    nc.scalar.copy(y[:, j, :], banks[h][j][:])
                if j % 2 == 1:
                    nc.sync.dma_start(out_rows[:, j - 1:j + 1, h * H:(h + 1) * H], y[:, j - 1:j + 1, :])
            for k in range(2):
                a, b = k * 256, (k + 1) * 256
                dst, src = weave_views(yw[:, a:b, :], y[:, :, a:b])
                if weave[k] == "v":
                    nc.vector.tensor_copy(dst, src)
                else:
                    nc.scalar.copy(dst, src)

        for u in range(2):
            for j in (2 * u, 2 * u + 1):
                negate_whole(0, j)
                for h in range(2):
                    look_up(0, j, h)
            for h in range(2):
                turn_and_add(0, u, h)
        err[1, 0] = keep.tile([P, L, H], F32, name="err10")
        look_up_pair(0)
        negate_pair(0, 0)
        turn_and_add(1, 0, 0, (0,))
        look_up_pair(1)
        negate_pair(1, 0)
        turn_and_add(1, 1, 0, (0,))
        turn_back(0, 0, where=(banks[0][0], banks[0][1]))
        weave_g(1, 0, 256, H, False)
        turn_back(1, 0, (0,), where=(banks[0][2],))
        turn_back(0, 1, where=(banks[0][3], banks[0][0]))
        look_up(1, 0, 1, tag="picked031")
        look_up(1, 1, 1, tag="z110")
        quantise_g(0, 0)
        multiply(0, 0)
        last = keep.tile([P, 2, H], F32, name="pickedlast", tag="gw00", align_bytes=64)
        for e in range(2):
            nc.vector.tensor_copy(last[:, e, :], book[1, 2 + e][:].indirect(offsets[:, 32:64]))
        quantise_g(1, 0)
        multiply(1, 0)
        finish(0, "ssss", "ss")
        err[1, 1] = keep.tile([P, L, H], F32, name="err11", tag="gw10", align_bytes=64)
        subtract(1, 0, 1, nc.vector)
        subtract(1, 1, 1, nc.vector)
        nc.vector.tensor_tensor(err[1, 1][:, 2:4, :], zpair[1, 1][:], last[:], SUB)
        quantise_g(0, 1, tag="z110")
        multiply(0, 1)
        weave_g(1, 1, 0, H, True)
        quantise_g(1, 1)
        multiply(1, 1)
        finish(1, "vsvs", "vs")
        for k, tag in enumerate(("gw11", "gc11")):
            codes = keep.tile([P, 256], U32, name=f"y_codes0{k}", tag=tag, align_bytes=64)
            quantise_y(0, k, codes[:])
            nc.sync.dma_start(codes_out[:, 256 * k:256 * (k + 1)], codes[:].bitcast(I32))
        codes = keep.tile([P, H], U32, name="y_codes1", align_bytes=64)
        for k in range(2):
            quantise_y(1, k, codes[:, 256 * k:256 * (k + 1)])
        nc.sync.dma_start(codes_out[:, H:T], codes[:].bitcast(I32))
        for q in range(4):
            eng = nc.sync if q % 2 == 0 else nc.scalar
            eng.dma_start(out_2[0, 4 * q:4 * q + 4, :].bitcast(I32), y_scales[32 * q:32 * q + 4, :].bitcast(I32))
